import numpy as np, ml_dtypes
CORES = [40,41,42,43,44,45,46,47]
N = 8
BF = ml_dtypes.bfloat16
def f(rng, *shape):
    return (rng.standard_normal(shape, dtype=np.float32) * np.exp2(rng.integers(-2, 3, shape[:-1] + (1,)))).astype(BF)
def wide(rng, *shape):
    v = f(rng, *shape).astype(np.float32); k = shape[:-2] + (1, shape[-1])
    return (v * np.exp2(rng.integers(-6, 7, k)) * (rng.random(k) > 0.0625)).astype(BF)
def gentries(a):
    return np.ascontiguousarray(a.reshape(8, 16, -1).transpose(0, 2, 1)).reshape(8, -1)
def gtable(e):
    e = np.asarray(e); return np.ascontiguousarray(e.reshape(8, -1, 16).transpose(0, 2, 1)).reshape(128, -1).astype(np.int32)
W, F, U, CAP, SW = 6, 64, 3, 8, 2
C = W * F; Z = C + (W - 1) * N * CAP
def pack(x):
    return np.stack([gtable(v.reshape(8, -1)) for v in x])
def unpack(x):
    return np.stack([gentries(v) for v in x])
def sends(rng, full):
    x = np.argsort(rng.random((N, 8, W - 1, N, F)), axis=-1)[..., :CAP] + F * np.arange(W - 1).reshape(1, 1, W - 1, 1, 1)
    n = rng.integers(0, CAP + 1, (N, 8, W - 1, N, 1)); n[0, :, 0, 1] = CAP
    if full: n[:] = CAP
    keep = (np.argsort(rng.random(x.shape), axis=-1) < n) & (np.arange(N).reshape(N, 1, 1, 1, 1) != np.arange(N).reshape(1, 1, 1, N, 1))
    return np.where(keep, x, Z)
def upwind(rng, far, none):
    s = (N, 8, W, U, F); r = np.arange(N).reshape(N, 1, 1, 1, 1); w = np.arange(W).reshape(1, 1, W, 1, 1)
    v = np.where(rng.random(s) < 0.75, w - 1, (rng.random(s) * w).astype(np.int64))
    near = v * F + rng.integers(0, F, s); away = C + (v * N + (r + 1 + rng.integers(0, N - 1, s)) % N) * CAP + rng.integers(0, CAP, s)
    p = rng.random(s)
    return np.where(w == 0, Z, np.where(p < far, away, np.where(p < far + none, Z, near)))
def draw(rng, o, p, x):
    return {"qs": f(rng, N, 128, C), "rm": (0.5 + 0.5 * rng.random((N, 128, C))).astype(BF), "co": (0.75 * rng.random((N, 128, U * C))).astype(BF),
            "sc": (f(rng, N, 16, 16).astype(np.float32) * np.float32(0.0625)).astype(BF), "seq": pack(o), "up": pack(p), "snd": pack(x)}
def orders(rng):
    return np.argsort(rng.random((N, 8, C)), axis=-1)
def setup_inputs(rng):
    return draw(rng, orders(rng), upwind(rng, 0.5, 0.1), sends(rng, False))
def setup_inputs_full(rng):
    return draw(rng, orders(rng), upwind(rng, 0.9, 0.0), sends(rng, True))
def setup_inputs_chain(rng):
    w = np.arange(W).reshape(1, 1, W, 1, 1); r = np.arange(N).reshape(N, 1, 1, 1, 1); x = sends(rng, True)
    p = np.where(w == 0, Z, C + ((w - 1) * N + (r + 1) % N) * CAP + rng.integers(0, CAP, (N, 8, W, U, F)))
    other = np.arange(N).reshape(N, 1, 1, 1) != np.arange(N).reshape(1, 1, 1, N); a = F * np.arange(W - 1).reshape(1, 1, W - 1, 1)
    x[..., 0] = np.where(other, a, Z); x[..., CAP - 1] = np.where(other, a + F - 1, Z)
    return draw(rng, orders(rng), p, x)
def setup_inputs_alike(rng):
    x = sends(rng, True); x[:] = x[..., :1].copy(); p = upwind(rng, 0.5, 0.1); p = np.repeat(p[:, :, :, :1], U, axis=3)
    o = orders(rng); o[:, 0] = np.arange(C); o[:, 1] = np.arange(C)[::-1]; o[:, 3] = o[:, 2]
    return draw(rng, o, p, x)
def setup_inputs_few(rng):
    x = sends(rng, False); k = int(rng.integers(0, N)); x[k] = Z; x[:, :, :, k] = Z
    d = draw(rng, orders(rng), upwind(rng, 0.08, 0.85), x); d["rm"] = np.where(rng.random(d["rm"].shape) < 0.125, np.float32(0), d["rm"].astype(np.float32)).astype(BF)
    return d
def setup_inputs_spread(rng):
    d = setup_inputs(rng); d["qs"] = wide(rng, N, 128, C); return d
def check_inputs(d):
    bad = []
    if not (np.sort(unpack(d["seq"]), axis=-1) == np.arange(C)).all(): bad.append("seq")
    p = unpack(d["up"]).reshape(N, 8, W, U * F).astype(np.int64); w = np.arange(W).reshape(1, 1, W, 1); r = np.arange(N).reshape(N, 1, 1, 1); s = p - C
    if not ((p == Z) | ((p >= 0) & (p < w * F)) | ((s >= 0) & (s < w * N * CAP) & ((s // CAP) % N != r))).all(): bad.append("up")
    x = unpack(d["snd"]).reshape(N, 8, W - 1, N, CAP).astype(np.int64); w = np.arange(W - 1).reshape(1, 1, W - 1, 1, 1)
    other = np.arange(N).reshape(N, 1, 1, 1, 1) != np.arange(N).reshape(1, 1, 1, N, 1)
    if not ((x == Z) | ((x >= w * F) & (x < w * F + F) & other)).all(): bad.append("snd")
    if not all(np.isfinite(d[k].astype(np.float32)).all() for k in ("qs", "rm", "co", "sc")): bad.append("finite")
    return bad
def reference(qs, rm, co, sc, seq, up, snd):
    o = unpack(seq).astype(np.int64); p = unpack(up).astype(np.int64); x = unpack(snd).astype(np.int64)
    src = qs.astype(np.float64).reshape(N, 8, 16, C); rem = rm.astype(np.float64).reshape(N, 8, 16, C); a = co.astype(np.float64).reshape(N, 8, 16, W, U, F)
    s = sc.astype(np.float64).transpose(0, 2, 1); y = np.zeros((N, 16, C), np.float64)
    for k in range(SW):
        win = np.zeros((N, 8, 16, Z + 1), np.float64)
        for w in range(W):
            c = o[:, :, None, w * F:w * F + F]
            h = np.take_along_axis(win, p[:, :, None, w * U * F:(w + 1) * U * F], 3).reshape(N, 8, 16, U, F)
            v = (np.take_along_axis(src, c, 3) + np.sum(a[:, :, :, w] * h, axis=3)) * np.take_along_axis(rem, c, 3)
            win[..., w * F:w * F + F] = v
            if w == W - 1: continue
            for r in range(N):
                for q in range(N):
                    if q == r: continue
                    b = C + (w * N + r) * CAP; e = (w * N + q) * CAP
                    win[q, :, :, b:b + CAP] = np.take_along_axis(win[r], x[r][:, None, e:e + CAP], 2)
        psi = np.zeros((N, 8, 16, C), np.float64); np.put_along_axis(psi, o[:, :, None], win[..., :C], 3)
        flux = np.sum(psi, axis=1); y = flux
        src = np.repeat(np.matmul(s, flux)[:, None], 8, axis=1)
    return {"y": y.astype(np.float32)}

@@ -1,0 +1,215 @@
+from concourse.bass import DstId, RemoteDMATransfer
+from concourse.mybir import AluOpType as A
+
+W, F, U, CAP, SW, N = 6, 64, 3, 8, 2, 8
+C = W * F
+B = F + CAP + N * CAP
+WIN = (W - 1) * B + F + CAP
+NCH, CH = 3, 128
+
+SCRATCH = {
+    "seqi": ("sbuf", [128, 24], "int32"), "sndi": ("sbuf", [128, 20], "int32"), "upi": ("sbuf", [128, 72], "int32"),
+    "qb": ("sbuf", [128, C], "bfloat16"), "rb": ("sbuf", [128, C], "bfloat16"), "cb": ("sbuf", [128, U * C], "bfloat16"),
+    "scb": ("sbuf", [128, 16], "bfloat16"),
+    "seq16": ("sbuf", [128, 24], "uint16"), "snd16": ("sbuf", [128, 20], "uint16"), "up16": ("sbuf", [128, 72], "uint16"),
+    "k0": ("sbuf", [128, 72], "int32"), "k1": ("sbuf", [128, 72], "int32"), "k2": ("sbuf", [128, 72], "int32"),
+    "rp": ("sbuf", [128, C], "float32"), "a": ("sbuf", [128, U * C], "float32"), "b": ("sbuf", [128, C], "float32"),
+    "win0": ("sbuf", [128, WIN], "float32"), "win1": ("sbuf", [128, WIN], "float32"),
+    "prod": ("sbuf", [128, U * F], "float32"), "t2": ("sbuf", [128, F], "float32"),
+    "sent": ("sbuf", [128, SW * (W - 1) * F], "float32"),
+    "fl0": ("sbuf", [128, C], "float32"), "fl1": ("sbuf", [128, C], "float32"), "ss": ("sbuf", [128, C], "float32"),
+    "ysb": ("sbuf", [128, C], "float32"),
+    "i16": ("sbuf", [128, 16], "int32"), "d16": ("sbuf", [128, 16], "float32"),
+    "ir": ("sbuf", [128, 128], "int32"), "rr": ("sbuf", [128, 128], "bfloat16"),
+    "scw": ("sbuf", [128, 128], "bfloat16"), "sc8": ("sbuf", [128, 128], "float32"),
+    "bp": ("psum", [128, 512], "float32"), "tp": ("psum", [128, 512], "float32"), "scp": ("psum", [128, 512], "float32"),
+    "sp0": ("psum", [128, 512], "float32"), "sp1": ("psum", [128, 512], "float32"), "sp2": ("psum", [128, 512], "float32"),
+}
+LOADS = ["seq", "snd", "up", "sc", "rm", "qs", "co"]
+SEMAPHORES = (["ld_" + n for n in LOADS] + ["vs", "ps", "gs", "left", "st"]
+              + ["ar%d" % i for i in range(SW * (W - 1))])
+
+
+def lanes(core, peers, topo):
+    eng = topo.engines(core, peers[0])
+    for p in peers:
+        eng = [e for e in eng if e in topo.engines(core, p)]
+    per = 1
+    while per * 2 * len(peers) <= len(eng):
+        per *= 2
+    order = {True: eng[0::2] + eng[1::2], False: eng[1::2] + eng[0::2]}
+    used, out = [], {}
+    for p in sorted(peers, key=lambda p: topo.die(p) == topo.die(core)):
+        free = [e for e in order[topo.die(p) != topo.die(core)] if e not in used][:per]
+        used += free
+        out[p] = sum(1 << e for e in free)
+    return out, per
+
+
+def rank_program(g, core, T, topo):
+    rank = T.rank_of(core)
+    if rank is None:
+        return
+    v, s = g.vector, T.sem
+    for q, name, dst in ((g.sync, "seq", T.seqi), (g.scalar, "rm", T.rb), (g.sync, "snd", T.sndi), (g.scalar, "qs", T.qb),
+                         (g.sync, "up", T.upi), (g.scalar, "co", T.cb)):
+        q.dma_start(dst[:], T[name][:]).then_inc(s["ld_" + name], 16)
+    g.sync.dma_start(T.scb[0:16, :], T.sc[:]).then_inc(s.ld_sc, 16)
+    g.iota(T.i16[:], [[-1, 16]], 128, 1).then_inc(s.gs, 1)
+    g.iota(T.ir[0:16, :], [[-1, 128]], 128, 1).then_inc(s.gs, 1)
+
+    st = {"n": 0, "done": 0, "t": {}, "ext": {}}
+
+    def dep(*keys):
+        if max([st["t"].get(k, 0) for k in keys] + [0]) > st["done"]:
+            v.wait_ge(s.vs, st["n"])
+            st["done"] = st["n"]
+
+    def ext(name, val):
+        if st["ext"].get(name, 0) < val:
+            v.wait_ge(s[name], val)
+            st["ext"][name] = val
+
+    def op(ins, *touched):
+        ins.then_inc(s.vs, 1)
+        st["n"] += 1
+        for k in touched:
+            st["t"][k] = st["n"]
+        return st["n"]
+
+    def tt(out, in0, in1, o, rd, wr):
+        dep(*rd, *wr)
+        return op(v.tensor_tensor(out, in0, in1, o), *rd, *wr)
+
+    def ts(out, in0, s1, s2, o0, o1, rd, wr):
+        dep(*rd, *wr)
+        if o1 is None:
+            return op(v.tensor_scalar(out, in0, s1, None, o0), *rd, *wr)
+        return op(v.tensor_scalar(out, in0, s1, s2, o0, o1), *rd, *wr)
+
+    def cp(out, in_, rd, wr):
+        dep(*rd, *wr)
+        return op(v.tensor_copy(out, in_), *rd, *wr)
+
+    wins = (T.win0, T.win1)
+    for k in range(SW):
+        for w in range(W - 1):
+            z, o = w * B + F, w * B + F + CAP + rank * CAP
+            if rank == 0:
+                op(v.memset(wins[k][:, z:z + 2 * CAP], 0.0), "win%d" % k)
+            else:
+                op(v.memset(wins[k][:, z:z + CAP], 0.0), "win%d" % k)
+                op(v.memset(wins[k][:, o:o + CAP], 0.0), "win%d" % k)
+
+    peers = [c for c in T.cores if c != core]
+    masks, per = lanes(core, peers, topo)
+    off = lambda t, w, k: t[:, k * w:k * w + k]
+
+    def ship(k, w):
+        i = k * (W - 1) + w
+        wn, key = wins[k], "win%d" % k
+        n = cp(T.sent[:, i * F:i * F + F], wn[:, w * B:w * B + F + CAP].indirect(off(T.snd16, w, 4)), [key, "snd16"], ["sent"])
+        g.wait_ge(s.vs, n)
+        tr = []
+        for p in peers:
+            rid, pid, _ = topo.addr(p)
+            d = T.rank_of(p)
+            c0 = w * B + F + CAP + rank * CAP
+            tr.append(RemoteDMATransfer(dst_ids=[DstId(rid=rid, pnc=pid)], dma_engine_mask=masks[p], remote_sem=s["ar%d" % i],
+                                        src=T.sent[:, i * F + d * CAP:i * F + d * CAP + CAP], dst=wn[:, c0:c0 + CAP]))
+        g.remote_dma_fused(tr, local_sem=s.left)
+
+    def scat(k, w):
+        cp((T.fl0, T.fl1)[k][:].indirect(off(T.seq16, w, 4)), wins[k][:, w * B:w * B + F], ["win%d" % k, "seq16"], ["fl%d" % k])
+
+    def coef(w):
+        for u in range(U):
+            j = (w * U + u) * F
+            tt(T.a[:, j:j + F], T.cb[:, j:j + F], T.rp[:, w * F:w * F + F], A.mult, ["rp"], ["a"])
+
+    ext("ld_seq", 16)
+    cp(T.seq16[:], T.seqi[:], [], ["seq16"])
+    ext("ld_rm", 16)
+    cp(T.rp[:, 0:F], T.rb[:].indirect(off(T.seq16, 0, 4)), ["seq16"], ["rp"])
+    ext("ld_snd", 16)
+    ts(T.snd16[:, 0:4], T.sndi[:, 0:4], F, None, A.min, None, [], ["snd16"])
+    ext("ld_qs", 16)
+    tt(T.win0[:, 0:F], T.qb[:].indirect(off(T.seq16, 0, 4)), T.rp[:, 0:F], A.mult, ["rp", "seq16"], ["win0"])
+    ship(0, 0)
+    ext("ld_up", 16)
+    L, K0, K1, K2 = (t[:, 12:72] for t in (T.upi, T.k0, T.k1, T.k2))
+    ts(K0, L, 6, None, A.arith_shift_right, None, [], ["k0"])
+    ts(K1, L, C, -(6 * B - F - CAP), A.is_ge, A.mult, [], ["k1"])
+    ts(K2, L, C + (W - 1) * N * CAP, -(5 * B + F + CAP - F), A.is_ge, A.mult, [], ["k2"])
+    ts(K0, K0, B - F, 0, A.mult, A.add, [], ["k0"])
+    tt(K1, K1, K2, A.add, ["k2"], ["k1"])
+    tt(K0, K0, L, A.add, [], ["k0"])
+    tt(K0, K0, K1, A.add, ["k1"], ["k0"])
+    cp(T.up16[:, 12:72], K0, ["k0"], ["up16"])
+    cp(T.rp[:, F:C], T.rb[:].indirect(T.seq16[:, 4:24]), ["seq16"], ["rp"])
+    tt(T.b[:, F:C], T.qb[:].indirect(T.seq16[:, 4:24]), T.rp[:, F:C], A.mult, ["rp", "seq16"], ["b"])
+    ext("ld_co", 16)
+    coef(1)
+    cp(T.bp[:, F:C], T.b[:, F:C], ["b"], ["bp"])
+
+    def later(w):
+        if w < W - 1:
+            coef(w + 1)
+        if w == 1:
+            for x in range(2, W - 1):
+                ts(T.snd16[:, 4 * x:4 * x + 4], T.sndi[:, 4 * x:4 * x + 4], -F * x, F, A.add, A.min, [], ["snd16"])
+            ext("gs", 2)
+            ts(T.i16[:], T.i16[:], 15, None, A.bitwise_and, None, [], ["i16"])
+            ts(T.ir[0:16, :], T.ir[0:16, :], 15, None, A.bitwise_and, None, [], ["ir"])
+            ts(T.d16[:], T.i16[:], 0, None, A.is_equal, None, ["i16"], ["d16"])
+            ts(T.rr[0:16, :], T.ir[0:16, :], 0, None, A.is_equal, None, ["ir"], ["rr"])
+            ext("ld_sc", 16)
+            for x in range(8):
+                n = cp(T.scw[0:16, 16 * x:16 * x + 16], T.scb[0:16, :], [], ["scw%d" % x])
+            g.tensor.wait_ge(s.vs, n)
+            g.tensor.matmul(T.scp[:, 0:128], T.rr[0:16, :], T.scw[0:16, :], True, True).then_inc(s.ps, 1)
+        if w == 2:
+            ext("ps", 1)
+            cp(T.sc8[:], T.scp[:, 0:128], [], ["sc8"])
+
+    ts(T.snd16[:, 4:8], T.sndi[:, 4:8], -F, F, A.add, A.min, [], ["snd16"])
+    scat(0, 0)
+    sp = (T.sp0, T.sp1, T.sp2)
+    for k in range(SW):
+        wn, key = wins[k], "win%d" % k
+        if k:
+            g.tensor.wait_ge(s.vs, st["n"])
+            for c in range(NCH):
+                g.tensor.matmul(sp[c][:, 0:CH], T.sc8[:], T.fl0[:, c * CH:c * CH + CH], True, True).then_inc(s.ps, 1)
+            for c in range(NCH):
+                ext("ps", 2 + c)
+                cp(T.ss[:, c * CH:c * CH + CH], sp[c][:, 0:CH], [], ["ss"] if c == NCH - 1 else [])
+            tt(wn[:, 0:F], T.ss[:].indirect(off(T.seq16, 0, 4)), T.rp[:, 0:F], A.mult, ["ss"], [key])
+            ship(k, 0)
+            tt(T.b[:, F:C], T.ss[:].indirect(T.seq16[:, 4:24]), T.rp[:, F:C], A.mult, ["ss"], ["b"])
+            cp(T.bp[:, F:C], T.b[:, F:C], ["b"], ["bp"])
+            scat(k, 0)
+        for w in range(1, W):
+            ext("ar%d" % (k * (W - 1) + w - 1), per * len(peers))
+            tt(T.prod[:], wn[:, 0:w * B].indirect(off(T.up16, w, 12)), T.a[:, w * U * F:(w + 1) * U * F], A.mult,
+               [key, "up16", "a"], ["prod"])
+            tt(T.tp[:, 0:F], T.prod[:, 0:F], T.prod[:, F:2 * F], A.add, ["prod"], ["tp"])
+            if max(st["t"]["bp"], 0) > st["done"]:
+                dep("bp")
+            op(v.tensor_tensor(T.t2[:], T.prod[:, 2 * F:3 * F], T.bp[:, w * F:w * F + F], A.add), "t2", "prod", "bp")
+            tt(wn[:, w * B:w * B + F], T.tp[:, 0:F], T.t2[:], A.add, ["tp", "t2"], [key])
+            if w < W - 1:
+                ship(k, w)
+                if k == 0:
+                    later(w)
+            scat(k, w)
+    g.tensor.wait_ge(s.vs, st["n"])
+    for c in range(NCH):
+        g.tensor.matmul(sp[c][0:16, 0:CH], T.d16[:], T.fl1[:, c * CH:c * CH + CH], True, True).then_inc(s.ps, 1)
+    for c in range(NCH):
+        ext("ps", 2 + NCH + c)
+        n = cp(T.ysb[0:16, c * CH:c * CH + CH], sp[c][0:16, 0:CH], [], ["y%d" % c])
+    g.sync.wait_ge(s.vs, n)
+    g.sync.dma_start(T.y[:], T.ysb[0:16, :]).then_inc(s.st, 16)
+    g.sync.wait_ge(s.st, 16)
+    g.wait_ge(s.left, per * len(peers) * SW * (W - 1))

@@ -1,32 +1,32 @@
 from concourse.bass import DstId, RemoteDMATransfer
-from concourse.mybir import AluOpType as A
+from concourse.mybir import AluOpType as A, ActivationFunctionType as AF
 
 W, F, U, CAP, SW, N = 6, 64, 3, 8, 2, 8
 C = W * F
-B = F + CAP + N * CAP
-WIN = (W - 1) * B + F + CAP
-NCH, CH = 3, 128
+Z = C + (W - 1) * N * CAP
+ZERO = (W - 1) * F
+NCH = 3
+CUT = (0, 160, 320, C)
 
 SCRATCH = {
     "seqi": ("sbuf", [128, 24], "int32"), "sndi": ("sbuf", [128, 20], "int32"), "upi": ("sbuf", [128, 72], "int32"),
     "qb": ("sbuf", [128, C], "bfloat16"), "rb": ("sbuf", [128, C], "bfloat16"), "cb": ("sbuf", [128, U * C], "bfloat16"),
     "scb": ("sbuf", [128, 16], "bfloat16"),
     "seq16": ("sbuf", [128, 24], "uint16"), "snd16": ("sbuf", [128, 20], "uint16"), "up16": ("sbuf", [128, 72], "uint16"),
-    "k0": ("sbuf", [128, 72], "int32"), "k1": ("sbuf", [128, 72], "int32"), "k2": ("sbuf", [128, 72], "int32"),
-    "rp": ("sbuf", [128, C], "float32"), "a": ("sbuf", [128, U * C], "float32"), "b": ("sbuf", [128, C], "float32"),
-    "win0": ("sbuf", [128, WIN], "float32"), "win1": ("sbuf", [128, WIN], "float32"),
-    "prod": ("sbuf", [128, U * F], "float32"), "t2": ("sbuf", [128, F], "float32"),
+    "k0": ("sbuf", [128, 72], "int32"),
+    "rp": ("sbuf", [128, C], "float32"), "b": ("sbuf", [128, C], "float32"), "a": ("sbuf", [128, U * C], "float32"),
+    "win0": ("sbuf", [128, Z], "float32"), "win1": ("sbuf", [128, Z], "float32"),
+    "prod": ("sbuf", [128, U * F], "float32"), "t1": ("sbuf", [128, F], "float32"), "t2": ("sbuf", [128, F], "float32"),
     "sent": ("sbuf", [128, SW * (W - 1) * F], "float32"),
     "fl0": ("sbuf", [128, C], "float32"), "fl1": ("sbuf", [128, C], "float32"), "ss": ("sbuf", [128, C], "float32"),
-    "ysb": ("sbuf", [128, C], "float32"),
-    "i16": ("sbuf", [128, 16], "int32"), "d16": ("sbuf", [128, 16], "float32"),
-    "ir": ("sbuf", [128, 128], "int32"), "rr": ("sbuf", [128, 128], "bfloat16"),
-    "scw": ("sbuf", [128, 128], "bfloat16"), "sc8": ("sbuf", [128, 128], "float32"),
+    "ysb": ("sbuf", [128, 96], "float32"),
+    "im": ("sbuf", [128, 128], "int32"), "mk": ("sbuf", [128, 128], "float32"),
+    "scw": ("sbuf", [128, 128], "float32"), "sc8": ("sbuf", [128, 128], "float32"),
     "bp": ("psum", [128, 512], "float32"), "tp": ("psum", [128, 512], "float32"), "scp": ("psum", [128, 512], "float32"),
     "sp0": ("psum", [128, 512], "float32"), "sp1": ("psum", [128, 512], "float32"), "sp2": ("psum", [128, 512], "float32"),
 }
 LOADS = ["seq", "snd", "up", "sc", "rm", "qs", "co"]
-SEMAPHORES = (["ld_" + n for n in LOADS] + ["vs", "ps", "gs", "left", "st"]
+SEMAPHORES = (["ld_" + n for n in LOADS] + ["vs", "ps", "acs", "gs", "left", "st"]
               + ["ar%d" % i for i in range(SW * (W - 1))])
 
 
@@ -55,13 +55,12 @@ def rank_program(g, core, T, topo):
                          (g.sync, "up", T.upi), (g.scalar, "co", T.cb)):
         q.dma_start(dst[:], T[name][:]).then_inc(s["ld_" + name], 16)
     g.sync.dma_start(T.scb[0:16, :], T.sc[:]).then_inc(s.ld_sc, 16)
-    g.iota(T.i16[:], [[-1, 16]], 128, 1).then_inc(s.gs, 1)
-    g.iota(T.ir[0:16, :], [[-1, 128]], 128, 1).then_inc(s.gs, 1)
+    g.iota(T.im[:], [[1, 128]], 128, -1).then_inc(s.gs, 1)
 
-    st = {"n": 0, "done": 0, "t": {}, "ext": {}}
+    st = {"n": 0, "done": 0, "t": {}, "w": {}, "ext": {}, "act": 0}
 
-    def dep(*keys):
-        if max([st["t"].get(k, 0) for k in keys] + [0]) > st["done"]:
+    def dep(rd, wr):
+        if max([st["w"].get(k, 0) for k in rd] + [st["t"].get(k, 0) for k in wr] + [0]) > st["done"]:
             v.wait_ge(s.vs, st["n"])
             st["done"] = st["n"]
 
@@ -70,146 +69,161 @@ def rank_program(g, core, T, topo):
             v.wait_ge(s[name], val)
             st["ext"][name] = val
 
-    def op(ins, *touched):
+    def op(ins, rd, wr):
         ins.then_inc(s.vs, 1)
         st["n"] += 1
-        for k in touched:
+        for k in rd + wr:
             st["t"][k] = st["n"]
+        for k in wr:
+            st["w"][k] = st["n"]
         return st["n"]
 
     def tt(out, in0, in1, o, rd, wr):
-        dep(*rd, *wr)
-        return op(v.tensor_tensor(out, in0, in1, o), *rd, *wr)
+        dep(rd, wr)
+        return op(v.tensor_tensor(out, in0, in1, o), rd, wr)
 
     def ts(out, in0, s1, s2, o0, o1, rd, wr):
-        dep(*rd, *wr)
+        dep(rd, wr)
         if o1 is None:
-            return op(v.tensor_scalar(out, in0, s1, None, o0), *rd, *wr)
-        return op(v.tensor_scalar(out, in0, s1, s2, o0, o1), *rd, *wr)
+            return op(v.tensor_scalar(out, in0, s1, None, o0), rd, wr)
+        return op(v.tensor_scalar(out, in0, s1, s2, o0, o1), rd, wr)
 
     def cp(out, in_, rd, wr):
-        dep(*rd, *wr)
-        return op(v.tensor_copy(out, in_), *rd, *wr)
+        dep(rd, wr)
+        return op(v.tensor_copy(out, in_), rd, wr)
 
-    wins = (T.win0, T.win1)
-    for k in range(SW):
+    def act(out, in_, need=0):
+        if need:
+            g.scalar.wait_ge(s.vs, need)
+        g.scalar.activation(out, in_, AF.Copy).then_inc(s.acs, 1)
+        st["act"] += 1
+        return st["act"]
+
+    wins, fls = (T.win0, T.win1), (T.fl0, T.fl1)
+    off = lambda t, w, k: t[:, k * w:k * w + k]
+    cols = lambda t, w: t[:, w * F:w * F + F]
+    slot = lambda w, q: C + (w * N + q) * CAP
+
+    def zeros(k):
+        op(v.memset(wins[k][:, F:C], 0.0), [], ["win%d" % k])
         for w in range(W - 1):
-            z, o = w * B + F, w * B + F + CAP + rank * CAP
-            if rank == 0:
-                op(v.memset(wins[k][:, z:z + 2 * CAP], 0.0), "win%d" % k)
-            else:
-                op(v.memset(wins[k][:, z:z + CAP], 0.0), "win%d" % k)
-                op(v.memset(wins[k][:, o:o + CAP], 0.0), "win%d" % k)
+            op(v.memset(wins[k][:, slot(w, rank):slot(w, rank) + CAP], 0.0), [], ["win%d" % k])
 
     peers = [c for c in T.cores if c != core]
     masks, per = lanes(core, peers, topo)
-    off = lambda t, w, k: t[:, k * w:k * w + k]
 
     def ship(k, w):
         i = k * (W - 1) + w
-        wn, key = wins[k], "win%d" % k
-        n = cp(T.sent[:, i * F:i * F + F], wn[:, w * B:w * B + F + CAP].indirect(off(T.snd16, w, 4)), [key, "snd16"], ["sent"])
+        n = cp(cols(T.sent, i), wins[k][:, w * F:w * F + F + CAP].indirect(off(T.snd16, w, 4)), ["win%d" % k, "snd16%d" % w], [])
         g.wait_ge(s.vs, n)
         tr = []
         for p in peers:
             rid, pid, _ = topo.addr(p)
-            d = T.rank_of(p)
-            c0 = w * B + F + CAP + rank * CAP
+            c0 = i * F + T.rank_of(p) * CAP
             tr.append(RemoteDMATransfer(dst_ids=[DstId(rid=rid, pnc=pid)], dma_engine_mask=masks[p], remote_sem=s["ar%d" % i],
-                                        src=T.sent[:, i * F + d * CAP:i * F + d * CAP + CAP], dst=wn[:, c0:c0 + CAP]))
+                                        src=T.sent[:, c0:c0 + CAP], dst=wins[k][:, slot(w, rank):slot(w, rank) + CAP]))
         g.remote_dma_fused(tr, local_sem=s.left)
 
     def scat(k, w):
-        cp((T.fl0, T.fl1)[k][:].indirect(off(T.seq16, w, 4)), wins[k][:, w * B:w * B + F], ["win%d" % k, "seq16"], ["fl%d" % k])
+        cp(fls[k][:].indirect(off(T.seq16, w, 4)), cols(wins[k], w), ["win%d" % k, "seq16"], ["fl%d" % k])
 
     def coef(w):
         for u in range(U):
-            j = (w * U + u) * F
-            tt(T.a[:, j:j + F], T.cb[:, j:j + F], T.rp[:, w * F:w * F + F], A.mult, ["rp"], ["a"])
+            tt(cols(T.a, w * U + u), cols(T.cb, w * U + u), cols(T.rp, w), A.mult, [], ["a%d" % w])
 
+    abp = {}
+
+    def source(k, w):
+        src, key = ((T.qb, "qb"), (T.ss, "ss"))[k]
+        n = tt(cols(T.b, w), src[:].indirect(off(T.seq16, w, 4)), cols(T.rp, w), A.mult, [key, "seq16"], ["b%d" % w])
+        abp[w] = act(cols(T.bp, w), cols(T.b, w), n)
+
+    zeros(0)
+    ext("gs", 1)
+    ts(T.im[:], T.im[:], 15, None, A.bitwise_and, None, [], ["im"])
+    nmk = ts(T.mk[:], T.im[:], 0, None, A.is_equal, None, ["im"], ["mk"])
     ext("ld_seq", 16)
-    cp(T.seq16[:], T.seqi[:], [], ["seq16"])
+    nseq = cp(T.seq16[:], T.seqi[:], [], ["seq16"])
     ext("ld_rm", 16)
     cp(T.rp[:, 0:F], T.rb[:].indirect(off(T.seq16, 0, 4)), ["seq16"], ["rp"])
     ext("ld_snd", 16)
-    ts(T.snd16[:, 0:4], T.sndi[:, 0:4], F, None, A.min, None, [], ["snd16"])
+    ts(T.snd16[:, 0:4], T.sndi[:, 0:4], F, None, A.min, None, [], ["snd160"])
     ext("ld_qs", 16)
     tt(T.win0[:, 0:F], T.qb[:].indirect(off(T.seq16, 0, 4)), T.rp[:, 0:F], A.mult, ["rp", "seq16"], ["win0"])
     ship(0, 0)
+    g.scalar.wait_ge(s.ld_rm, 16)
+    arp1 = act(T.rp[:, F:2 * F], T.rb[:].indirect(T.seq16[:, 4:8]), nseq)
     ext("ld_up", 16)
-    L, K0, K1, K2 = (t[:, 12:72] for t in (T.upi, T.k0, T.k1, T.k2))
-    ts(K0, L, 6, None, A.arith_shift_right, None, [], ["k0"])
-    ts(K1, L, C, -(6 * B - F - CAP), A.is_ge, A.mult, [], ["k1"])
-    ts(K2, L, C + (W - 1) * N * CAP, -(5 * B + F + CAP - F), A.is_ge, A.mult, [], ["k2"])
-    ts(K0, K0, B - F, 0, A.mult, A.add, [], ["k0"])
-    tt(K1, K1, K2, A.add, ["k2"], ["k1"])
-    tt(K0, K0, L, A.add, [], ["k0"])
-    tt(K0, K0, K1, A.add, ["k1"], ["k0"])
+    L, K0 = T.upi[:, 12:72], T.k0[:, 12:72]
+    ts(K0, L, Z, ZERO - Z, A.is_ge, A.mult, [], ["k0"])
+    tt(K0, K0, L, A.add, ["k0"], ["k0"])
     cp(T.up16[:, 12:72], K0, ["k0"], ["up16"])
-    cp(T.rp[:, F:C], T.rb[:].indirect(T.seq16[:, 4:24]), ["seq16"], ["rp"])
-    tt(T.b[:, F:C], T.qb[:].indirect(T.seq16[:, 4:24]), T.rp[:, F:C], A.mult, ["rp", "seq16"], ["b"])
+    ext("acs", arp1)
+    source(0, 1)
+    arp2 = act(T.rp[:, 2 * F:], T.rb[:].indirect(T.seq16[:, 8:24]))
     ext("ld_co", 16)
     coef(1)
-    cp(T.bp[:, F:C], T.b[:, F:C], ["b"], ["bp"])
+    g.scalar.wait_ge(s.ld_sc, 16)
+    for x in range(8):
+        asc = act(T.scw[0:16, 16 * x:16 * x + 16], T.scb[0:16, :])
+    g.tensor.wait_ge(s.vs, nmk)
+    g.tensor.wait_ge(s.acs, asc)
+    g.tensor.matmul(T.scp[:, 0:128], T.mk[0:16, :], T.scw[0:16, :], True, True).then_inc(s.ps, 1)
+    g.scalar.wait_ge(s.ps, 1)
+    asc8 = act(T.sc8[:], T.scp[:, 0:128])
 
-    def later(w):
-        if w < W - 1:
-            coef(w + 1)
-        if w == 1:
-            for x in range(2, W - 1):
-                ts(T.snd16[:, 4 * x:4 * x + 4], T.sndi[:, 4 * x:4 * x + 4], -F * x, F, A.add, A.min, [], ["snd16"])
-            ext("gs", 2)
-            ts(T.i16[:], T.i16[:], 15, None, A.bitwise_and, None, [], ["i16"])
-            ts(T.ir[0:16, :], T.ir[0:16, :], 15, None, A.bitwise_and, None, [], ["ir"])
-            ts(T.d16[:], T.i16[:], 0, None, A.is_equal, None, ["i16"], ["d16"])
-            ts(T.rr[0:16, :], T.ir[0:16, :], 0, None, A.is_equal, None, ["ir"], ["rr"])
-            ext("ld_sc", 16)
-            for x in range(8):
-                n = cp(T.scw[0:16, 16 * x:16 * x + 16], T.scb[0:16, :], [], ["scw%d" % x])
-            g.tensor.wait_ge(s.vs, n)
-            g.tensor.matmul(T.scp[:, 0:128], T.rr[0:16, :], T.scw[0:16, :], True, True).then_inc(s.ps, 1)
-        if w == 2:
-            ext("ps", 1)
-            cp(T.sc8[:], T.scp[:, 0:128], [], ["sc8"])
+    def ahead(k, w):
+        if k == 0 and w < W - 2:
+            ts(off(T.snd16, w + 1, 4), off(T.sndi, w + 1, 4), -F * (w + 1), F, A.add, A.min, [], ["snd16%d" % (w + 1)])
+        if (k, w) != (0, 0):
+            if k == 0:
+                ext("acs", arp2)
+            source(k, w + 1)
+            if k == 0:
+                coef(w + 1)
+        scat(k, w)
 
-    ts(T.snd16[:, 4:8], T.sndi[:, 4:8], -F, F, A.add, A.min, [], ["snd16"])
-    scat(0, 0)
+    ahead(0, 0)
     sp = (T.sp0, T.sp1, T.sp2)
     for k in range(SW):
         wn, key = wins[k], "win%d" % k
         if k:
             g.tensor.wait_ge(s.vs, st["n"])
+            g.tensor.wait_ge(s.acs, asc8)
             for c in range(NCH):
-                g.tensor.matmul(sp[c][:, 0:CH], T.sc8[:], T.fl0[:, c * CH:c * CH + CH], True, True).then_inc(s.ps, 1)
+                g.tensor.matmul(sp[c][:, 0:CUT[c + 1] - CUT[c]], T.sc8[:], T.fl0[:, CUT[c]:CUT[c + 1]], True, True).then_inc(s.ps, 1)
+            zeros(1)
             for c in range(NCH):
                 ext("ps", 2 + c)
-                cp(T.ss[:, c * CH:c * CH + CH], sp[c][:, 0:CH], [], ["ss"] if c == NCH - 1 else [])
+                op(v.tensor_copy(T.ss[:, CUT[c]:CUT[c + 1]], sp[c][:, 0:CUT[c + 1] - CUT[c]]), [], ["ss"])
             tt(wn[:, 0:F], T.ss[:].indirect(off(T.seq16, 0, 4)), T.rp[:, 0:F], A.mult, ["ss"], [key])
             ship(k, 0)
-            tt(T.b[:, F:C], T.ss[:].indirect(T.seq16[:, 4:24]), T.rp[:, F:C], A.mult, ["ss"], ["b"])
-            cp(T.bp[:, F:C], T.b[:, F:C], ["b"], ["bp"])
-            scat(k, 0)
+            ahead(k, 0)
         for w in range(1, W):
+            dep([key, "up16", "a%d" % w], ["prod"])
+            ext("acs", abp[w])
             ext("ar%d" % (k * (W - 1) + w - 1), per * len(peers))
-            tt(T.prod[:], wn[:, 0:w * B].indirect(off(T.up16, w, 12)), T.a[:, w * U * F:(w + 1) * U * F], A.mult,
-               [key, "up16", "a"], ["prod"])
-            tt(T.tp[:, 0:F], T.prod[:, 0:F], T.prod[:, F:2 * F], A.add, ["prod"], ["tp"])
-            if max(st["t"]["bp"], 0) > st["done"]:
-                dep("bp")
-            op(v.tensor_tensor(T.t2[:], T.prod[:, 2 * F:3 * F], T.bp[:, w * F:w * F + F], A.add), "t2", "prod", "bp")
-            tt(wn[:, w * B:w * B + F], T.tp[:, 0:F], T.t2[:], A.add, ["tp", "t2"], [key])
-            if w < W - 1:
+            last = w == W - 1
+            o1, k1 = (T.t1[:], "t1") if last else (T.tp[:, 0:F], "tp")
+            tt(T.prod[:], wn[:, 0:C + w * N * CAP].indirect(off(T.up16, w, 12)), T.a[:, w * U * F:(w + 1) * U * F], A.mult,
+               [key, "up16", "a%d" % w], ["prod"])
+            tt(o1, cols(T.prod, 0), cols(T.prod, 1), A.add, ["prod"], [k1])
+            tt(T.t2[:], cols(T.prod, 2), cols(T.bp, w), A.add, ["prod"], ["t2"])
+            if last:
+                tt(fls[k][:].indirect(off(T.seq16, w, 4)), T.t1[:], T.t2[:], A.add, ["t1", "t2", "seq16"], ["fl%d" % k])
+            else:
+                tt(cols(wn, w), T.tp[:, 0:F], T.t2[:], A.add, ["tp", "t2"], [key])
                 ship(k, w)
-                if k == 0:
-                    later(w)
-            scat(k, w)
+                ahead(k, w)
     g.tensor.wait_ge(s.vs, st["n"])
     for c in range(NCH):
-        g.tensor.matmul(sp[c][0:16, 0:CH], T.d16[:], T.fl1[:, c * CH:c * CH + CH], True, True).then_inc(s.ps, 1)
+        g.tensor.matmul(sp[c][:, 0:32], T.fl1[:, c::NCH], T.mk[:, 0:32], True, True).then_inc(s.ps, 1)
     for c in range(NCH):
         ext("ps", 2 + NCH + c)
-        n = cp(T.ysb[0:16, c * CH:c * CH + CH], sp[c][0:16, 0:CH], [], ["y%d" % c])
-    g.sync.wait_ge(s.vs, n)
-    g.sync.dma_start(T.y[:], T.ysb[0:16, :]).then_inc(s.st, 16)
-    g.sync.wait_ge(s.st, 16)
+        n = op(v.transpose(T.ysb[:, c::NCH], sp[c][:, 0:32]), [], ["y"])
+    for i, q in enumerate((g.sync, g.scalar, g.sync, g.scalar)):
+        if i < 2:
+            q.wait_ge(s.vs, n)
+        q.dma_start(T.y[:, 96 * i:96 * i + 96], T.ysb[32 * i:32 * i + 16, :]).then_inc(s.st, 16)
+    g.sync.wait_ge(s.st, 64)
     g.wait_ge(s.left, per * len(peers) * SW * (W - 1))

@@ -5,6 +5,8 @@ W, F, U, CAP, SW, N = 6, 64, 3, 8, 2, 8
 C = W * F
 Z = C + (W - 1) * N * CAP
 ZERO = (W - 1) * F
+P = 8
+FP = F + P
 NCH = 3
 CUT = (0, 160, 320, C)
 
@@ -14,9 +16,11 @@ SCRATCH = {
     "scb": ("sbuf", [128, 16], "bfloat16"),
     "seq16": ("sbuf", [128, 24], "uint16"), "snd16": ("sbuf", [128, 20], "uint16"), "up16": ("sbuf", [128, 72], "uint16"),
     "k0": ("sbuf", [128, 72], "int32"),
-    "rp": ("sbuf", [128, C], "float32"), "b": ("sbuf", [128, C], "float32"), "a": ("sbuf", [128, U * C], "float32"),
+    "rp": ("sbuf", [128, C], "float32"), "b": ("sbuf", [128, W * FP], "float32"), "bs": ("sbuf", [128, C], "float32"),
+    "a": ("sbuf", [128, U * C], "float32"),
     "win0": ("sbuf", [128, Z], "float32"), "win1": ("sbuf", [128, Z], "float32"),
-    "prod": ("sbuf", [128, U * F], "float32"), "t1": ("sbuf", [128, F], "float32"), "t2": ("sbuf", [128, F], "float32"),
+    "prod": ("sbuf", [128, U * F + P], "float32"), "t1": ("sbuf", [128, FP], "float32"), "t2": ("sbuf", [128, F], "float32"),
+    "y3": ("sbuf", [128, F], "float32"),
     "sent": ("sbuf", [128, SW * (W - 1) * F], "float32"),
     "fl0": ("sbuf", [128, C], "float32"), "fl1": ("sbuf", [128, C], "float32"), "ss": ("sbuf", [128, C], "float32"),
     "ysb": ("sbuf", [128, 96], "float32"),
@@ -60,9 +64,10 @@ def rank_program(g, core, T, topo):
     st = {"n": 0, "done": 0, "t": {}, "w": {}, "ext": {}, "act": 0}
 
     def dep(rd, wr):
-        if max([st["w"].get(k, 0) for k in rd] + [st["t"].get(k, 0) for k in wr] + [0]) > st["done"]:
-            v.wait_ge(s.vs, st["n"])
-            st["done"] = st["n"]
+        need = max([st["w"].get(k, 0) for k in rd] + [st["t"].get(k, 0) for k in wr] + [0])
+        if need > st["done"]:
+            v.wait_ge(s.vs, need)
+            st["done"] = need
 
     def ext(name, val):
         if st["ext"].get(name, 0) < val:
@@ -92,6 +97,9 @@ def rank_program(g, core, T, topo):
         dep(rd, wr)
         return op(v.tensor_copy(out, in_), rd, wr)
 
+    def ms(ap, key):
+        return op(v.memset(ap, 0.0), [], [key])
+
     def act(out, in_, need=0):
         if need:
             g.scalar.wait_ge(s.vs, need)
@@ -105,16 +113,15 @@ def rank_program(g, core, T, topo):
     slot = lambda w, q: C + (w * N + q) * CAP
 
     def zeros(k):
-        op(v.memset(wins[k][:, F:C], 0.0), [], ["win%d" % k])
+        ms(wins[k][:, F:C], "win%d" % k)
         for w in range(W - 1):
-            op(v.memset(wins[k][:, slot(w, rank):slot(w, rank) + CAP], 0.0), [], ["win%d" % k])
+            ms(wins[k][:, slot(w, rank):slot(w, rank) + CAP], "win%d" % k)
 
     peers = [c for c in T.cores if c != core]
     masks, per = lanes(core, peers, topo)
 
-    def ship(k, w):
+    def ship(k, w, n):
         i = k * (W - 1) + w
-        n = cp(cols(T.sent, i), wins[k][:, w * F:w * F + F + CAP].indirect(off(T.snd16, w, 4)), ["win%d" % k, "snd16%d" % w], [])
         g.wait_ge(s.vs, n)
         tr = []
         for p in peers:
@@ -124,6 +131,9 @@ def rank_program(g, core, T, topo):
                                         src=T.sent[:, c0:c0 + CAP], dst=wins[k][:, slot(w, rank):slot(w, rank) + CAP]))
         g.remote_dma_fused(tr, local_sem=s.left)
 
+    def pick(k):
+        return cp(cols(T.sent, k * (W - 1)), wins[k][:, 0:FP].indirect(off(T.snd16, 0, 4)), ["win%d" % k, "snd160"], [])
+
     def scat(k, w):
         cp(fls[k][:].indirect(off(T.seq16, w, 4)), cols(wins[k], w), ["win%d" % k, "seq16"], ["fl%d" % k])
 
@@ -131,14 +141,25 @@ def rank_program(g, core, T, topo):
         for u in range(U):
             tt(cols(T.a, w * U + u), cols(T.cb, w * U + u), cols(T.rp, w), A.mult, [], ["a%d" % w])
 
-    abp = {}
+    abp, abs_ = {}, {}
 
     def source(k, w):
         src, key = ((T.qb, "qb"), (T.ss, "ss"))[k]
-        n = tt(cols(T.b, w), src[:].indirect(off(T.seq16, w, 4)), cols(T.rp, w), A.mult, [key, "seq16"], ["b%d" % w])
-        abp[w] = act(cols(T.bp, w), cols(T.b, w), n)
+        blk = T.b[:, w * FP:w * FP + FP]
+        n = tt(T.b[:, w * FP:w * FP + F], src[:].indirect(off(T.seq16, w, 4)), cols(T.rp, w), A.mult, [key, "seq16"], ["b%d" % w])
+        n = max(n, st["w"].get("snd16%d" % w, 0))
+        if w < W - 1:
+            abs_[w] = act(cols(T.bs, w), blk.indirect(off(T.snd16, w, 4)), n)
+            n = 0
+        abp[w] = act(cols(T.bp, w), T.b[:, w * FP:w * FP + F], n)
+
+    def snds(w):
+        ts(off(T.snd16, w, 4), off(T.sndi, w, 4), -F * w, F, A.add, A.min, [], ["snd16%d" % w])
 
     zeros(0)
+    ms(T.b[:, FP:], "b")
+    ms(T.prod[:, U * F:], "pz")
+    ms(T.t1[:, F:], "tz")
     ext("gs", 1)
     ts(T.im[:], T.im[:], 15, None, A.bitwise_and, None, [], ["im"])
     nmk = ts(T.mk[:], T.im[:], 0, None, A.is_equal, None, ["im"], ["mk"])
@@ -147,22 +168,24 @@ def rank_program(g, core, T, topo):
     ext("ld_rm", 16)
     cp(T.rp[:, 0:F], T.rb[:].indirect(off(T.seq16, 0, 4)), ["seq16"], ["rp"])
     ext("ld_snd", 16)
-    ts(T.snd16[:, 0:4], T.sndi[:, 0:4], F, None, A.min, None, [], ["snd160"])
+    snds(0)
     ext("ld_qs", 16)
     tt(T.win0[:, 0:F], T.qb[:].indirect(off(T.seq16, 0, 4)), T.rp[:, 0:F], A.mult, ["rp", "seq16"], ["win0"])
-    ship(0, 0)
+    snds(1)
+    ship(0, 0, pick(0))
     g.scalar.wait_ge(s.ld_rm, 16)
     arp1 = act(T.rp[:, F:2 * F], T.rb[:].indirect(T.seq16[:, 4:8]), nseq)
     ext("ld_up", 16)
     L, K0 = T.upi[:, 12:72], T.k0[:, 12:72]
     ts(K0, L, Z, ZERO - Z, A.is_ge, A.mult, [], ["k0"])
-    tt(K0, K0, L, A.add, ["k0"], ["k0"])
-    cp(T.up16[:, 12:72], K0, ["k0"], ["up16"])
     ext("acs", arp1)
     source(0, 1)
-    arp2 = act(T.rp[:, 2 * F:], T.rb[:].indirect(T.seq16[:, 8:24]))
+    tt(K0, K0, L, A.add, ["k0"], ["k0"])
+    scat(0, 0)
+    cp(T.up16[:, 12:72], K0, ["k0"], ["up16"])
     ext("ld_co", 16)
     coef(1)
+    arp2 = act(T.rp[:, 2 * F:], T.rb[:].indirect(T.seq16[:, 8:24]))
     g.scalar.wait_ge(s.ld_sc, 16)
     for x in range(8):
         asc = act(T.scw[0:16, 16 * x:16 * x + 16], T.scb[0:16, :])
@@ -174,16 +197,14 @@ def rank_program(g, core, T, topo):
 
     def ahead(k, w):
         if k == 0 and w < W - 2:
-            ts(off(T.snd16, w + 1, 4), off(T.sndi, w + 1, 4), -F * (w + 1), F, A.add, A.min, [], ["snd16%d" % (w + 1)])
-        if (k, w) != (0, 0):
-            if k == 0:
-                ext("acs", arp2)
-            source(k, w + 1)
-            if k == 0:
-                coef(w + 1)
+            snds(w + 1)
+        if k == 0:
+            ext("acs", arp2)
+        source(k, w + 1)
+        if k == 0:
+            coef(w + 1)
         scat(k, w)
 
-    ahead(0, 0)
     sp = (T.sp0, T.sp1, T.sp2)
     for k in range(SW):
         wn, key = wins[k], "win%d" % k
@@ -197,24 +218,33 @@ def rank_program(g, core, T, topo):
                 ext("ps", 2 + c)
                 op(v.tensor_copy(T.ss[:, CUT[c]:CUT[c + 1]], sp[c][:, 0:CUT[c + 1] - CUT[c]]), [], ["ss"])
             tt(wn[:, 0:F], T.ss[:].indirect(off(T.seq16, 0, 4)), T.rp[:, 0:F], A.mult, ["ss"], [key])
-            ship(k, 0)
+            ship(k, 0, pick(k))
             ahead(k, 0)
         for w in range(1, W):
-            dep([key, "up16", "a%d" % w], ["prod"])
-            ext("acs", abp[w])
+            dep([key, "up16", "a%d" % w], ["pa", "pb"])
             ext("ar%d" % (k * (W - 1) + w - 1), per * len(peers))
-            last = w == W - 1
-            o1, k1 = (T.t1[:], "t1") if last else (T.tp[:, 0:F], "tp")
-            tt(T.prod[:], wn[:, 0:C + w * N * CAP].indirect(off(T.up16, w, 12)), T.a[:, w * U * F:(w + 1) * U * F], A.mult,
-               [key, "up16", "a%d" % w], ["prod"])
-            tt(o1, cols(T.prod, 0), cols(T.prod, 1), A.add, ["prod"], [k1])
-            tt(T.t2[:], cols(T.prod, 2), cols(T.bp, w), A.add, ["prod"], ["t2"])
-            if last:
-                tt(fls[k][:].indirect(off(T.seq16, w, 4)), T.t1[:], T.t2[:], A.add, ["t1", "t2", "seq16"], ["fl%d" % k])
-            else:
-                tt(cols(wn, w), T.tp[:, 0:F], T.t2[:], A.add, ["tp", "t2"], [key])
-                ship(k, w)
-                ahead(k, w)
+            win = wn[:, 0:C + w * N * CAP]
+            j = w * U * F
+            if w == W - 1:
+                tt(T.prod[:, 0:U * F], win.indirect(off(T.up16, w, 12)), T.a[:, j:j + U * F], A.mult,
+                   [key, "up16", "a%d" % w], ["pa", "pb"])
+                tt(T.t1[:, 0:F], cols(T.prod, 0), cols(T.prod, 1), A.add, ["pb"], ["t1"])
+                ext("acs", abp[w])
+                tt(T.t2[:], cols(T.prod, 2), cols(T.bp, w), A.add, ["pa"], ["t2"])
+                tt(fls[k][:].indirect(off(T.seq16, w, 4)), T.t1[:, 0:F], T.t2[:], A.add, ["t1", "t2", "seq16"], ["fl%d" % k])
+                continue
+            lst = off(T.snd16, w, 4)
+            tt(cols(T.prod, 2), win.indirect(T.up16[:, 12 * w + 8:12 * w + 12]), T.a[:, j + 2 * F:j + 3 * F], A.mult,
+               [key, "up16", "a%d" % w], ["pa"])
+            tt(T.prod[:, 0:2 * F], win.indirect(T.up16[:, 12 * w:12 * w + 8]), T.a[:, j:j + 2 * F], A.mult,
+               [key, "up16", "a%d" % w], ["pb"])
+            ext("acs", abp[w])
+            tt(T.y3[:], T.prod[:, 2 * F:3 * F + P].indirect(lst), cols(T.bs, w), A.add, ["pa", "pz", "snd16%d" % w], ["y3"])
+            tt(T.t1[:, 0:F], cols(T.prod, 0), cols(T.prod, 1), A.add, ["pb"], ["t1"])
+            tt(T.tp[:, 0:F], cols(T.prod, 2), cols(T.bp, w), A.add, ["pa"], ["tp"])
+            ship(k, w, tt(cols(T.sent, k * (W - 1) + w), T.t1[:].indirect(lst), T.y3[:], A.add, ["t1", "tz", "y3"], []))
+            tt(cols(wn, w), T.t1[:, 0:F], T.tp[:, 0:F], A.add, ["t1", "tp"], [key])
+            ahead(k, w)
     g.tensor.wait_ge(s.vs, st["n"])
     for c in range(NCH):
         g.tensor.matmul(sp[c][:, 0:32], T.fl1[:, c::NCH], T.mk[:, 0:32], True, True).then_inc(s.ps, 1)

@@ -9,6 +9,7 @@ P = 8
 FP = F + P
 NCH = 3
 CUT = (0, 160, 320, C)
+H = N // 2
 
 SCRATCH = {
     "seqi": ("sbuf", [128, 24], "int32"), "sndi": ("sbuf", [128, 20], "int32"), "upi": ("sbuf", [128, 72], "int32"),
@@ -39,15 +40,9 @@ def lanes(core, peers, topo):
     for p in peers:
         eng = [e for e in eng if e in topo.engines(core, p)]
     per = 1
-    while per * 2 * len(peers) <= len(eng):
+    while per * 2 * H <= len(eng):
         per *= 2
-    order = {True: eng[0::2] + eng[1::2], False: eng[1::2] + eng[0::2]}
-    used, out = [], {}
-    for p in sorted(peers, key=lambda p: topo.die(p) == topo.die(core)):
-        free = [e for e in order[topo.die(p) != topo.die(core)] if e not in used][:per]
-        used += free
-        out[p] = sum(1 << e for e in free)
-    return out, per
+    return [sum(1 << e for e in eng[per * i:per * i + per]) for i in range(len(peers))], per
 
 
 def rank_program(g, core, T, topo):
@@ -117,22 +112,29 @@ def rank_program(g, core, T, topo):
         for w in range(W - 1):
             ms(wins[k][:, slot(w, rank):slot(w, rank) + CAP], "win%d" % k)
 
-    peers = [c for c in T.cores if c != core]
-    masks, per = lanes(core, peers, topo)
+    halves = (1 - rank // H, rank // H)
+    peers = [[c for c in T.cores[H * h:H * h + H] if c != core] for h in halves]
+    masks, per = lanes(core, peers[0], topo)
+    masks = [masks, lanes(core, peers[1], topo)[0]]
 
-    def ship(k, w, n):
+    def ship(k, w, half):
         i = k * (W - 1) + w
-        g.wait_ge(s.vs, n)
-        tr = []
-        for p in peers:
-            rid, pid, _ = topo.addr(p)
-            c0 = i * F + T.rank_of(p) * CAP
-            tr.append(RemoteDMATransfer(dst_ids=[DstId(rid=rid, pnc=pid)], dma_engine_mask=masks[p], remote_sem=s["ar%d" % i],
-                                        src=T.sent[:, c0:c0 + CAP], dst=wins[k][:, slot(w, rank):slot(w, rank) + CAP]))
-        g.remote_dma_fused(tr, local_sem=s.left)
+        for h, ps, ms_ in zip(halves, peers, masks):
+            n = half(T.snd16[:, 4 * w + 2 * h:4 * w + 2 * h + 2], slice(i * F + H * CAP * h, i * F + H * CAP * (h + 1)), H * CAP * h)
+            g.wait_ge(s.vs, n)
+            tr = []
+            for p, m in zip(ps, ms_):
+                rid, pid, _ = topo.addr(p)
+                c0 = i * F + T.rank_of(p) * CAP
+                tr.append(RemoteDMATransfer(dst_ids=[DstId(rid=rid, pnc=pid)], dma_engine_mask=m, remote_sem=s["ar%d" % i],
+                                            src=T.sent[:, c0:c0 + CAP], dst=wins[k][:, slot(w, rank):slot(w, rank) + CAP]))
+            g.remote_dma_fused(tr, local_sem=s.left)
 
-    def pick(k):
-        return cp(cols(T.sent, k * (W - 1)), wins[k][:, 0:FP].indirect(off(T.snd16, 0, 4)), ["win%d" % k, "snd160"], [])
+    def first(k):
+        return lambda lst, c, j: cp(T.sent[:, c], wins[k][:, 0:FP].indirect(lst), ["win%d" % k, "snd160"], [])
+
+    def later(w):
+        return lambda lst, c, j: tt(T.sent[:, c], T.t1[:].indirect(lst), T.y3[:, j:j + H * CAP], A.add, ["t1", "tz", "y3"], [])
 
     def scat(k, w):
         cp(fls[k][:].indirect(off(T.seq16, w, 4)), cols(wins[k], w), ["win%d" % k, "seq16"], ["fl%d" % k])
@@ -172,7 +174,7 @@ def rank_program(g, core, T, topo):
     ext("ld_qs", 16)
     tt(T.win0[:, 0:F], T.qb[:].indirect(off(T.seq16, 0, 4)), T.rp[:, 0:F], A.mult, ["rp", "seq16"], ["win0"])
     snds(1)
-    ship(0, 0, pick(0))
+    ship(0, 0, first(0))
     g.scalar.wait_ge(s.ld_rm, 16)
     arp1 = act(T.rp[:, F:2 * F], T.rb[:].indirect(T.seq16[:, 4:8]), nseq)
     ext("ld_up", 16)
@@ -218,11 +220,11 @@ def rank_program(g, core, T, topo):
                 ext("ps", 2 + c)
                 op(v.tensor_copy(T.ss[:, CUT[c]:CUT[c + 1]], sp[c][:, 0:CUT[c + 1] - CUT[c]]), [], ["ss"])
             tt(wn[:, 0:F], T.ss[:].indirect(off(T.seq16, 0, 4)), T.rp[:, 0:F], A.mult, ["ss"], [key])
-            ship(k, 0, pick(k))
+            ship(k, 0, first(k))
             ahead(k, 0)
         for w in range(1, W):
             dep([key, "up16", "a%d" % w], ["pa", "pb"])
-            ext("ar%d" % (k * (W - 1) + w - 1), per * len(peers))
+            ext("ar%d" % (k * (W - 1) + w - 1), per * (N - 1))
             win = wn[:, 0:C + w * N * CAP]
             j = w * U * F
             if w == W - 1:
@@ -242,7 +244,7 @@ def rank_program(g, core, T, topo):
             tt(T.y3[:], T.prod[:, 2 * F:3 * F + P].indirect(lst), cols(T.bs, w), A.add, ["pa", "pz", "snd16%d" % w], ["y3"])
             tt(T.t1[:, 0:F], cols(T.prod, 0), cols(T.prod, 1), A.add, ["pb"], ["t1"])
             tt(T.tp[:, 0:F], cols(T.prod, 2), cols(T.bp, w), A.add, ["pa"], ["tp"])
-            ship(k, w, tt(cols(T.sent, k * (W - 1) + w), T.t1[:].indirect(lst), T.y3[:], A.add, ["t1", "tz", "y3"], []))
+            ship(k, w, later(w))
             tt(cols(wn, w), T.t1[:, 0:F], T.tp[:, 0:F], A.add, ["t1", "tp"], [key])
             ahead(k, w)
     g.tensor.wait_ge(s.vs, st["n"])
@@ -256,4 +258,4 @@ def rank_program(g, core, T, topo):
             q.wait_ge(s.vs, n)
         q.dma_start(T.y[:, 96 * i:96 * i + 96], T.ysb[32 * i:32 * i + 16, :]).then_inc(s.st, 16)
     g.sync.wait_ge(s.st, 64)
-    g.wait_ge(s.left, per * len(peers) * SW * (W - 1))
+    g.wait_ge(s.left, per * (N - 1) * SW * (W - 1))

from concourse.bass import DstId, RemoteDMATransfer
from concourse.mybir import AluOpType as A, ActivationFunctionType as AF

W, F, U, CAP, SW, N = 6, 64, 3, 8, 2, 8
C = W * F
Z = C + (W - 1) * N * CAP
ZERO = (W - 1) * F
P = 8
FP = F + P
NCH = 3
CUT = (0, 160, 320, C)
H = N // 2

SCRATCH = {
    "seqi": ("sbuf", [128, 24], "int32"), "sndi": ("sbuf", [128, 20], "int32"), "upi": ("sbuf", [128, 72], "int32"),
    "qb": ("sbuf", [128, C], "bfloat16"), "rb": ("sbuf", [128, C], "bfloat16"), "cb": ("sbuf", [128, U * C], "bfloat16"),
    "scb": ("sbuf", [128, 16], "bfloat16"),
    "seq16": ("sbuf", [128, 24], "uint16"), "snd16": ("sbuf", [128, 20], "uint16"), "up16": ("sbuf", [128, 72], "uint16"),
    "k0": ("sbuf", [128, 72], "int32"),
    "rp": ("sbuf", [128, C], "float32"), "b": ("sbuf", [128, W * FP], "float32"), "bs": ("sbuf", [128, C], "float32"),
    "a": ("sbuf", [128, U * C], "float32"),
    "win0": ("sbuf", [128, Z], "float32"), "win1": ("sbuf", [128, Z], "float32"),
    "prod": ("sbuf", [128, U * F + P], "float32"), "t1": ("sbuf", [128, FP], "float32"), "t2": ("sbuf", [128, F], "float32"),
    "y3": ("sbuf", [128, F], "float32"),
    "sent": ("sbuf", [128, SW * (W - 1) * F], "float32"),
    "fl0": ("sbuf", [128, C], "float32"), "fl1": ("sbuf", [128, C], "float32"), "ss": ("sbuf", [128, C], "float32"),
    "ysb": ("sbuf", [128, 96], "float32"),
    "im": ("sbuf", [128, 128], "int32"), "mk": ("sbuf", [128, 128], "float32"),
    "scw": ("sbuf", [128, 128], "float32"), "sc8": ("sbuf", [128, 128], "float32"),
    "bp": ("psum", [128, 512], "float32"), "tp": ("psum", [128, 512], "float32"), "scp": ("psum", [128, 512], "float32"),
    "sp0": ("psum", [128, 512], "float32"), "sp1": ("psum", [128, 512], "float32"), "sp2": ("psum", [128, 512], "float32"),
}
LOADS = ["seq", "snd", "up", "sc", "rm", "qs", "co"]
SEMAPHORES = (["ld_" + n for n in LOADS] + ["vs", "ps", "acs", "gs", "left", "st"]
              + ["ar%d" % i for i in range(SW * (W - 1))])


def lanes(core, peers, topo):
    eng = topo.engines(core, peers[0])
    for p in peers:
        eng = [e for e in eng if e in topo.engines(core, p)]
    per = 1
    while per * 2 * H <= len(eng):
        per *= 2
    return [sum(1 << e for e in eng[per * i:per * i + per]) for i in range(len(peers))], per


def rank_program(g, core, T, topo):
    rank = T.rank_of(core)
    if rank is None:
        return
    v, s = g.vector, T.sem
    for q, name, dst in ((g.sync, "seq", T.seqi), (g.scalar, "rm", T.rb), (g.sync, "snd", T.sndi), (g.scalar, "qs", T.qb),
                         (g.sync, "up", T.upi), (g.scalar, "co", T.cb)):
        q.dma_start(dst[:], T[name][:]).then_inc(s["ld_" + name], 16)
    g.sync.dma_start(T.scb[0:16, :], T.sc[:]).then_inc(s.ld_sc, 16)
    g.iota(T.im[:], [[1, 128]], 128, -1).then_inc(s.gs, 1)

    st = {"n": 0, "done": 0, "t": {}, "w": {}, "ext": {}, "act": 0}

    def dep(rd, wr):
        need = max([st["w"].get(k, 0) for k in rd] + [st["t"].get(k, 0) for k in wr] + [0])
        if need > st["done"]:
            v.wait_ge(s.vs, need)
            st["done"] = need

    def ext(name, val):
        if st["ext"].get(name, 0) < val:
            v.wait_ge(s[name], val)
            st["ext"][name] = val

    def op(ins, rd, wr):
        ins.then_inc(s.vs, 1)
        st["n"] += 1
        for k in rd + wr:
            st["t"][k] = st["n"]
        for k in wr:
            st["w"][k] = st["n"]
        return st["n"]

    def tt(out, in0, in1, o, rd, wr):
        dep(rd, wr)
        return op(v.tensor_tensor(out, in0, in1, o), rd, wr)

    def ts(out, in0, s1, s2, o0, o1, rd, wr):
        dep(rd, wr)
        if o1 is None:
            return op(v.tensor_scalar(out, in0, s1, None, o0), rd, wr)
        return op(v.tensor_scalar(out, in0, s1, s2, o0, o1), rd, wr)

    def cp(out, in_, rd, wr):
        dep(rd, wr)
        return op(v.tensor_copy(out, in_), rd, wr)

    def ms(ap, key):
        return op(v.memset(ap, 0.0), [], [key])

    def act(out, in_, need=0):
        if need:
            g.scalar.wait_ge(s.vs, need)
        g.scalar.activation(out, in_, AF.Copy).then_inc(s.acs, 1)
        st["act"] += 1
        return st["act"]

    wins, fls = (T.win0, T.win1), (T.fl0, T.fl1)
    off = lambda t, w, k: t[:, k * w:k * w + k]
    cols = lambda t, w: t[:, w * F:w * F + F]
    slot = lambda w, q: C + (w * N + q) * CAP

    def zeros(k):
        ms(wins[k][:, F:C], "win%d" % k)
        for w in range(W - 1):
            ms(wins[k][:, slot(w, rank):slot(w, rank) + CAP], "win%d" % k)

    halves = (1 - rank // H, rank // H)
    peers = [[c for c in T.cores[H * h:H * h + H] if c != core] for h in halves]
    masks, per = lanes(core, peers[0], topo)
    masks = [masks, lanes(core, peers[1], topo)[0]]

    def ship(k, w, half):
        i = k * (W - 1) + w
        for h, ps, ms_ in zip(halves, peers, masks):
            n = half(T.snd16[:, 4 * w + 2 * h:4 * w + 2 * h + 2], slice(i * F + H * CAP * h, i * F + H * CAP * (h + 1)), H * CAP * h)
            g.wait_ge(s.vs, n)
            tr = []
            for p, m in zip(ps, ms_):
                rid, pid, _ = topo.addr(p)
                c0 = i * F + T.rank_of(p) * CAP
                tr.append(RemoteDMATransfer(dst_ids=[DstId(rid=rid, pnc=pid)], dma_engine_mask=m, remote_sem=s["ar%d" % i],
                                            src=T.sent[:, c0:c0 + CAP], dst=wins[k][:, slot(w, rank):slot(w, rank) + CAP]))
            g.remote_dma_fused(tr, local_sem=s.left)

    def first(k):
        return lambda lst, c, j: cp(T.sent[:, c], wins[k][:, 0:FP].indirect(lst), ["win%d" % k, "snd160"], [])

    def later(w):
        return lambda lst, c, j: tt(T.sent[:, c], T.t1[:].indirect(lst), T.y3[:, j:j + H * CAP], A.add, ["t1", "tz", "y3"], [])

    def scat(k, w):
        cp(fls[k][:].indirect(off(T.seq16, w, 4)), cols(wins[k], w), ["win%d" % k, "seq16"], ["fl%d" % k])

    def coef(w):
        for u in range(U):
            tt(cols(T.a, w * U + u), cols(T.cb, w * U + u), cols(T.rp, w), A.mult, [], ["a%d" % w])

    abp, abs_ = {}, {}

    def source(k, w):
        src, key = ((T.qb, "qb"), (T.ss, "ss"))[k]
        blk = T.b[:, w * FP:w * FP + FP]
        n = tt(T.b[:, w * FP:w * FP + F], src[:].indirect(off(T.seq16, w, 4)), cols(T.rp, w), A.mult, [key, "seq16"], ["b%d" % w])
        n = max(n, st["w"].get("snd16%d" % w, 0))
        if w < W - 1:
            abs_[w] = act(cols(T.bs, w), blk.indirect(off(T.snd16, w, 4)), n)
            n = 0
        abp[w] = act(cols(T.bp, w), T.b[:, w * FP:w * FP + F], n)

    def snds(w):
        ts(off(T.snd16, w, 4), off(T.sndi, w, 4), -F * w, F, A.add, A.min, [], ["snd16%d" % w])

    zeros(0)
    ms(T.b[:, FP:], "b")
    ms(T.prod[:, U * F:], "pz")
    ms(T.t1[:, F:], "tz")
    ext("gs", 1)
    ts(T.im[:], T.im[:], 15, None, A.bitwise_and, None, [], ["im"])
    nmk = ts(T.mk[:], T.im[:], 0, None, A.is_equal, None, ["im"], ["mk"])
    ext("ld_seq", 16)
    nseq = cp(T.seq16[:], T.seqi[:], [], ["seq16"])
    ext("ld_rm", 16)
    cp(T.rp[:, 0:F], T.rb[:].indirect(off(T.seq16, 0, 4)), ["seq16"], ["rp"])
    ext("ld_snd", 16)
    snds(0)
    ext("ld_qs", 16)
    tt(T.win0[:, 0:F], T.qb[:].indirect(off(T.seq16, 0, 4)), T.rp[:, 0:F], A.mult, ["rp", "seq16"], ["win0"])
    snds(1)
    ship(0, 0, first(0))
    g.scalar.wait_ge(s.ld_rm, 16)
    arp1 = act(T.rp[:, F:2 * F], T.rb[:].indirect(T.seq16[:, 4:8]), nseq)
    ext("ld_up", 16)
    L, K0 = T.upi[:, 12:72], T.k0[:, 12:72]
    ts(K0, L, Z, ZERO - Z, A.is_ge, A.mult, [], ["k0"])
    ext("acs", arp1)
    source(0, 1)
    tt(K0, K0, L, A.add, ["k0"], ["k0"])
    scat(0, 0)
    cp(T.up16[:, 12:72], K0, ["k0"], ["up16"])
    ext("ld_co", 16)
    coef(1)
    arp2 = act(T.rp[:, 2 * F:], T.rb[:].indirect(T.seq16[:, 8:24]))
    g.scalar.wait_ge(s.ld_sc, 16)
    for x in range(8):
        asc = act(T.scw[0:16, 16 * x:16 * x + 16], T.scb[0:16, :])
    g.tensor.wait_ge(s.vs, nmk)
    g.tensor.wait_ge(s.acs, asc)
    g.tensor.matmul(T.scp[:, 0:128], T.mk[0:16, :], T.scw[0:16, :], True, True).then_inc(s.ps, 1)
    g.scalar.wait_ge(s.ps, 1)
    asc8 = act(T.sc8[:], T.scp[:, 0:128])

    def ahead(k, w):
        if k == 0 and w < W - 2:
            snds(w + 1)
        if k == 0:
            ext("acs", arp2)
        source(k, w + 1)
        if k == 0:
            coef(w + 1)
        scat(k, w)

    sp = (T.sp0, T.sp1, T.sp2)
    for k in range(SW):
        wn, key = wins[k], "win%d" % k
        if k:
            g.tensor.wait_ge(s.vs, st["n"])
            g.tensor.wait_ge(s.acs, asc8)
            for c in range(NCH):
                g.tensor.matmul(sp[c][:, 0:CUT[c + 1] - CUT[c]], T.sc8[:], T.fl0[:, CUT[c]:CUT[c + 1]], True, True).then_inc(s.ps, 1)
            zeros(1)
            for c in range(NCH):
                ext("ps", 2 + c)
                op(v.tensor_copy(T.ss[:, CUT[c]:CUT[c + 1]], sp[c][:, 0:CUT[c + 1] - CUT[c]]), [], ["ss"])
            tt(wn[:, 0:F], T.ss[:].indirect(off(T.seq16, 0, 4)), T.rp[:, 0:F], A.mult, ["ss"], [key])
            ship(k, 0, first(k))
            ahead(k, 0)
        for w in range(1, W):
            dep([key, "up16", "a%d" % w], ["pa", "pb"])
            ext("ar%d" % (k * (W - 1) + w - 1), per * (N - 1))
            win = wn[:, 0:C + w * N * CAP]
            j = w * U * F
            if w == W - 1:
                tt(T.prod[:, 0:U * F], win.indirect(off(T.up16, w, 12)), T.a[:, j:j + U * F], A.mult,
                   [key, "up16", "a%d" % w], ["pa", "pb"])
                tt(T.t1[:, 0:F], cols(T.prod, 0), cols(T.prod, 1), A.add, ["pb"], ["t1"])
                ext("acs", abp[w])
                tt(T.t2[:], cols(T.prod, 2), cols(T.bp, w), A.add, ["pa"], ["t2"])
                tt(fls[k][:].indirect(off(T.seq16, w, 4)), T.t1[:, 0:F], T.t2[:], A.add, ["t1", "t2", "seq16"], ["fl%d" % k])
                continue
            lst = off(T.snd16, w, 4)
            tt(cols(T.prod, 2), win.indirect(T.up16[:, 12 * w + 8:12 * w + 12]), T.a[:, j + 2 * F:j + 3 * F], A.mult,
               [key, "up16", "a%d" % w], ["pa"])
            tt(T.prod[:, 0:2 * F], win.indirect(T.up16[:, 12 * w:12 * w + 8]), T.a[:, j:j + 2 * F], A.mult,
               [key, "up16", "a%d" % w], ["pb"])
            ext("acs", abp[w])
            tt(T.y3[:], T.prod[:, 2 * F:3 * F + P].indirect(lst), cols(T.bs, w), A.add, ["pa", "pz", "snd16%d" % w], ["y3"])
            tt(T.t1[:, 0:F], cols(T.prod, 0), cols(T.prod, 1), A.add, ["pb"], ["t1"])
            tt(T.tp[:, 0:F], cols(T.prod, 2), cols(T.bp, w), A.add, ["pa"], ["tp"])
            ship(k, w, later(w))
            tt(cols(wn, w), T.t1[:, 0:F], T.tp[:, 0:F], A.add, ["t1", "tp"], [key])
            ahead(k, w)
    g.tensor.wait_ge(s.vs, st["n"])
    for c in range(NCH):
        g.tensor.matmul(sp[c][:, 0:32], T.fl1[:, c::NCH], T.mk[:, 0:32], True, True).then_inc(s.ps, 1)
    for c in range(NCH):
        ext("ps", 2 + NCH + c)
        n = op(v.transpose(T.ysb[:, c::NCH], sp[c][:, 0:32]), [], ["y"])
    for i, q in enumerate((g.sync, g.scalar, g.sync, g.scalar)):
        if i < 2:
            q.wait_ge(s.vs, n)
        q.dma_start(T.y[:, 96 * i:96 * i + 96], T.ysb[32 * i:32 * i + 16, :]).then_inc(s.st, 16)
    g.sync.wait_ge(s.st, 64)
    g.wait_ge(s.left, per * (N - 1) * SW * (W - 1))
